import numpy as np
import ml_dtypes


def mxq(x, axis, fmt="e4m3"):
    dtype, down = {"e4m3": (ml_dtypes.float8_e4m3fn, 7), "e5m2": (ml_dtypes.float8_e5m2, 14)}[fmt]
    v = np.moveaxis(np.asarray(x, np.float32).astype(ml_dtypes.bfloat16).astype(np.float64), axis, -1)
    blocks = v.reshape(v.shape[:-1] + (-1, 32))
    amax = np.abs(blocks).max(-1, keepdims=True)
    byte = np.maximum(np.where(amax > 0, np.frexp(amax)[1] - 1 + 127, 0) - down, 1)
    scale = np.exp2(byte - 127.0)
    codes = (blocks / scale).astype(np.float32).astype(dtype).astype(np.float64)
    return np.moveaxis((codes * scale).reshape(v.shape), -1, axis)


WIDE = False


def mx_kscale(k):
    if not WIDE:
        return np.ones(k)
    levels = np.array([10, -10, 5, -5, 0])
    if k % 512:
        return np.exp2(np.random.permutation(np.resize(levels, k // 32))).repeat(32)
    a = np.empty((k // 512, 16))
    for p in range(k // 512):
        a[p, :8] = np.random.permutation(np.resize(levels, 8))
        for g in range(8):
            far = levels[np.abs(levels - a[p, g]) >= 10]
            a[p, g + 8] = far[np.random.randint(len(far))]
    return np.exp2(a.ravel()).repeat(32)


def f64(x):
    return np.asarray(x).astype(np.float64)


def striped(idx):
    return np.tile(idx.reshape(-1, 16).T, (8, 1)).astype(np.uint16)


def unstriped(offs):
    return offs[:16].T.reshape(-1).astype(np.int64)


E2M1 = np.array([0.0, 0.5, 1.0, 1.5, 2.0, 3.0, 4.0, 6.0, -0.0, -0.5, -1.0, -1.5, -2.0, -3.0, -4.0, -6.0])


def pack_weight(w, fmt):
    k, n = w.shape
    w = f64(np.asarray(w, np.float32).astype(ml_dtypes.bfloat16)).reshape(k // 32, 32, n)
    amax = np.abs(w).max(1)
    if fmt == "e4m3":
        byte = np.frexp(amax)[1] - 1 + 127 - 7
    else:
        mant, ex = np.frexp(amax / 6.0)
        byte = np.where(mant > 0.5, ex, ex - 1) + 127
    byte = np.clip(np.where(amax > 0, byte, 1), 1, 254)
    scaled = (w * np.exp2(127.0 - byte)[:, None, :]).reshape(k, n).astype(np.float32)
    by_word = np.ascontiguousarray(scaled.reshape(k // 512, 128, 4, n).transpose(0, 1, 3, 2))
    if fmt == "e4m3":
        words = by_word.astype(ml_dtypes.float8_e4m3fn).view(np.uint8)
    else:
        c = by_word.astype(ml_dtypes.float4_e2m1fn).view(np.uint8) & 0xF
        words = (c[..., 0::2] | (c[..., 1::2] << 4)).reshape(k // 512, 128, 2 * n)
    return np.ascontiguousarray(words), np.ascontiguousarray(byte.astype(np.uint8).reshape(k // 512, 16, n))


def unpack_weight(words, scales, fmt):
    g, _, n = scales.shape
    words = np.ascontiguousarray(words).reshape(g, 128, n, -1)
    if fmt == "e4m3":
        vals = words.view(ml_dtypes.float8_e4m3fn).astype(np.float64)
    else:
        nib = np.empty((g, 128, n, 4), np.uint8)
        nib[..., 0::2] = words & 0xF
        nib[..., 1::2] = words >> 4
        vals = E2M1[nib]
    vals = vals * np.repeat(np.exp2(scales.astype(np.float64) - 127.0), 8, axis=1)[..., None]
    return vals.transpose(0, 1, 3, 2).reshape(g * 512, n)


def gelu(v):
    return 0.5 * v * (1.0 + np.tanh(np.sqrt(2.0 / np.pi) * (v + 0.044715 * v**3)))


K, T, E, H, N = 512, 2048, 4, 512, 512
COUNTS = (128, 256, 640, 1024)
STARTS = np.cumsum((0,) + COUNTS)


def by_expert(wq, xq):
    return np.concatenate([wq[e].T @ xq[:, STARTS[e]:STARTS[e + 1]] for e in range(E)], axis=1)


def setup_inputs():
    n = np.random.standard_normal
    s = mx_kscale(K)[:, None]
    u = mx_kscale(H)
    expert = np.random.permutation(np.repeat(np.arange(E), COUNTS))
    slot_token = np.argsort(expert, kind="stable")
    w1 = [pack_weight(m, "e2m1") for m in n((E, K, H)) / np.sqrt(K) / s[None]]
    w3 = [pack_weight(m, "e2m1") for m in n((E, K, H)) / np.sqrt(K) / s[None] * u[None, None, :]]
    w2 = [pack_weight(m, "e2m1") for m in n((E, H, N)) / np.sqrt(H) / u[None, :, None]]
    return {
        "xT": (n((K, T)) * s).astype(np.float32),
        "w1_words": np.stack([m[0] for m in w1]),
        "w1_scales": np.stack([m[1] for m in w1]),
        "w3_words": np.stack([m[0] for m in w3]),
        "w3_scales": np.stack([m[1] for m in w3]),
        "w2_words": np.stack([m[0] for m in w2]),
        "w2_scales": np.stack([m[1] for m in w2]),
        "gate": np.tile(np.random.uniform(0.2, 1.0, T), (N, 1)).astype(np.float32),
        "offs": striped(slot_token),
    }


def reference(xT, w1_words, w1_scales, w3_words, w3_scales, w2_words, w2_scales, gate, offs):
    idx = unstriped(offs)
    w1 = np.stack([unpack_weight(w1_words[e], w1_scales[e], "e2m1") for e in range(E)])
    w3 = np.stack([unpack_weight(w3_words[e], w3_scales[e], "e2m1") for e in range(E)])
    w2 = np.stack([unpack_weight(w2_words[e], w2_scales[e], "e2m1") for e in range(E)])
    xq = mxq(f64(xT)[:, idx], 0, "e4m3")
    h = gelu(by_expert(w1, xq))
    h = h * by_expert(w3, xq)
    y = by_expert(w2, mxq(h, 0, "e4m3"))
    out = np.zeros((N, T))
    out[:, idx] = f64(gate) * y
    return out

@@ -1,0 +1,245 @@
+from contextlib import ExitStack
+
+import concourse.mybir as mybir
+from concourse.masks import make_identity
+
+K, T, E, H, N = 512, 2048, 4, 512, 512
+COUNTS = (128, 256, 640, 1024)
+
+FLOPS = 3 * 2 * K * H * T
+BYTES = 4 * K * T + 3 * E * (K * H // 2 + K * H // 32) + 4 * T + 2 * T * 8 + 4 * N * T
+
+F32 = mybir.dt.float32
+BF16 = mybir.dt.bfloat16
+I32 = mybir.dt.int32
+U32 = mybir.dt.uint32
+U16 = mybir.dt.uint16
+U8 = mybir.dt.uint8
+FP8X4 = mybir.dt.float8_e4m3fn_x4
+FP4X4 = mybir.dt.float4_e2m1fn_x4
+COPY = mybir.ActivationFunctionType.Copy
+GELU = mybir.ActivationFunctionType.Gelu_apprx_tanh
+MULT = mybir.AluOpType.mult
+
+P = 128
+CHUNK = 512
+VECTOR_COLS = 320
+GATHERS = (256, 384, 384, 512, 512)
+PIECE = 512
+
+
+def tile_moe_rag_glu_gelu_kernel(
+    tc, xT, w1_words, w1_scales, w3_words, w3_scales, w2_words, w2_scales, gate, offs, out
+):
+    nc = tc.nc
+    tiles = T // P
+    expert_of = [e for e in range(E) for i in range(COUNTS[e] // P)]
+
+    with ExitStack() as ctx:
+        held = ctx.enter_context(tc.tile_pool(name="held", bufs=1))
+        raws = ctx.enter_context(tc.tile_pool(name="raws", bufs=4))
+        stage = ctx.enter_context(tc.tile_pool(name="stage", bufs=3))
+        psum_ab = ctx.enter_context(tc.psum_pool(name="psum_ab", bufs=2))
+        psum_y = ctx.enter_context(tc.psum_pool(name="psum_y", bufs=2))
+        psum_t = ctx.enter_context(tc.psum_pool(name="psum_t", bufs=1))
+
+        offsets = held.tile([P, T // 16], U16, name="offsets")
+        x_words = held.tile([P, T], U32, name="x_words", align_bytes=64)
+        x_scales = held.tile([P, T], U8, name="x_scales", align_bytes=64)
+        nc.gpsimd.memset(x_scales[:], 0)
+
+        warm = held.tile([P, 8], F32, name="warm")
+        nc.vector.memset(warm[:], 0.0)
+        nc.scalar.activation(warm[:, 0:1], warm[:, 1:2], GELU)
+
+        planes = []
+        for name in ("w1", "w3", "w2"):
+            plane = held.tile([P, E, H], U8, name="plane_" + name, align_bytes=64)
+            nc.vector.memset(plane[:].rearrange("p e n -> p (e n)").bitcast(I32), 0)
+            planes.append(plane)
+        gate_rows = held.tile([P, P], F32, name="gate_rows")
+        nc.vector.memset(gate_rows[:], 0.0)
+
+        x_view = xT.rearrange("(p j) w -> p j w", j=4)
+        raw_tiles = []
+        for c in range(T // CHUNK):
+            raw = raws.tile([P, 4, CHUNK], F32, name="raw")
+            nc.sync.dma_start(raw[:], x_view[:, :, c * CHUNK:(c + 1) * CHUNK])
+            raw_tiles.append(raw)
+            if c == 1:
+                nc.sync.dma_start(offsets[:], offs)
+
+        def load_scales(plane, scales):
+            view = scales.rearrange("e s q n -> q (e s) n")
+            for quad in range(4):
+                nc.sync.dma_start(
+                    plane[32 * quad:32 * quad + 4, :, :].bitcast(I32),
+                    view[4 * quad:4 * quad + 4, :, :].bitcast(I32),
+                )
+
+        def load_words(tile, words, lo, hi):
+            view = words.rearrange("e s p n -> p (e s) n")
+            nc.sync.dma_start(tile[:, lo:hi, :].bitcast(I32), view[:, lo:hi, :].bitcast(I32))
+
+        w1 = held.tile([P, E, 2 * H], U8, name="w1", align_bytes=64)
+        w3 = held.tile([P, E, 2 * H], U8, name="w3", align_bytes=64)
+        w2 = held.tile([P, E, 2 * N], U8, name="w2", align_bytes=64)
+        load_scales(planes[0], w1_scales)
+        load_scales(planes[1], w3_scales)
+        load_words(w1, w1_words, 0, 2)
+        load_words(w3, w3_words, 0, 2)
+        load_words(w1, w1_words, 2, 4)
+        load_words(w3, w3_words, 2, 4)
+        load_scales(planes[2], w2_scales)
+        load_words(w2, w2_words, 0, 4)
+        nc.scalar.dma_start(gate_rows[0:tiles, :], gate[0:1, :].rearrange("o (c p) -> (o c) p", p=P))
+
+        identity = held.tile([P, P], F32, name="identity")
+        make_identity(nc, identity[:])
+
+        for c in range(T // CHUNK):
+            raw = raw_tiles[c]
+            grouped = stage.tile([P, CHUNK, 4], BF16, name="grouped", align_bytes=64)
+            for lo, hi, copy in ((0, VECTOR_COLS, nc.vector.tensor_copy), (VECTOR_COLS, CHUNK, nc.scalar.copy)):
+                copy(
+                    grouped[:, lo:hi, :].rearrange("p (c i) j -> p c j i", i=4),
+                    raw[:, :, lo:hi].rearrange("p j (c i) -> p c j i", i=4),
+                )
+            cols = slice(c * CHUNK, (c + 1) * CHUNK)
+            nc.vector.quantize_mx(
+                out=x_words[:, cols].bitcast(FP8X4),
+                scales=x_scales[:, cols],
+                in_=grouped[:].rearrange("p w j -> p (w j)"),
+            )
+
+        gate_psum = psum_t.tile([P, P], F32, name="yt")
+        nc.tensor.transpose(gate_psum[:], gate_rows[:], identity[:])
+        gates = held.tile([P, tiles], F32, name="gates")
+        nc.vector.tensor_copy(gates[:], gate_psum[:, 0:tiles])
+
+        slot_words, slot_scales = [], []
+
+        def gather(g):
+            lo = sum(GATHERS[:g])
+            n = GATHERS[g]
+            words = held.tile([P, n], U32, name="slot_words%d" % g, align_bytes=64)
+            scales = held.tile([P, n], U8, name="slot_scales%d" % g, align_bytes=64)
+            picked = offsets[:, lo // 16:(lo + n) // 16]
+            nc.vector.tensor_copy(words[:], x_words[:].indirect(picked))
+            nc.vector.tensor_copy(scales[:], x_scales[:].indirect(picked))
+            for k in range(n // P):
+                slot_words.append(words[:, k * P:(k + 1) * P])
+                slot_scales.append(scales[:, k * P:(k + 1) * P])
+
+        hidden_words, hidden_scales = [], []
+
+        def first_layer(pair):
+            turned = psum_t.tile([P, 2, 2, P], F32, name="ht")
+            for i in range(2):
+                t = 2 * pair + i
+                e = expert_of[t]
+                sums = []
+                for w, plane, name in ((w1, planes[0], "a"), (w3, planes[1], "b")):
+                    acc = psum_ab.tile([P, H], F32, name=name)
+                    nc.tensor.matmul_mx(
+                        out=acc[:],
+                        lhsT=slot_words[t].bitcast(FP8X4),
+                        lhsT_scale=slot_scales[t],
+                        rhs=w[:, e, :].bitcast(FP4X4),
+                        rhs_scale=plane[:, e, :],
+                        start=True,
+                        stop=True,
+                    )
+                    sums.append(acc)
+                g = stage.tile([P, H], F32, name="g")
+                nc.scalar.activation(g[:], sums[0][:], GELU)
+                h = stage.tile([P, H], BF16, name="h")
+                nc.vector.tensor_tensor(h[:], g[:], sums[1][:], MULT)
+                pairs = h[:].bitcast(F32)
+                for u in range(2):
+                    nc.tensor.transpose(turned[:, i, u, :], pairs[:, u::2], identity[:])
+            grouped = stage.tile([P, 2 * P * 4], BF16, name="hg", align_bytes=64)
+            nc.scalar.copy(
+                grouped[:].bitcast(F32).rearrange("p (k r u) -> p k r u", k=2, u=2),
+                turned[:].rearrange("p k u r -> p k r u"),
+            )
+            words = held.tile([P, 2 * P], U32, name="h_words%d" % pair, align_bytes=64)
+            scales = held.tile([P, 2 * P], U8, name="h_scales%d" % pair, align_bytes=64)
+            nc.vector.quantize_mx(out=words[:].bitcast(FP8X4), scales=scales[:], in_=grouped[:])
+            for i in range(2):
+                hidden_words.append(words[:, i * P:(i + 1) * P])
+                hidden_scales.append(scales[:, i * P:(i + 1) * P])
+
+        results = {}
+
+        def second_layer(t):
+            e = expert_of[t]
+            acc = psum_y.tile([P, N], F32, name="y")
+            nc.tensor.matmul_mx(
+                out=acc[:],
+                lhsT=hidden_words[t].bitcast(FP8X4),
+                lhsT_scale=hidden_scales[t],
+                rhs=w2[:, e, :].bitcast(FP4X4),
+                rhs_scale=planes[2][:, e, :],
+                start=True,
+                stop=True,
+            )
+            y = stage.tile([P, N], F32, name="y_tokens")
+            nc.scalar.activation(y[:], acc[:], COPY, scale=gates[:, t:t + 1])
+            back = psum_t.tile([P, 4, P], F32, name="yt")
+            for b in range(4):
+                nc.tensor.transpose(back[:, b, :], y[:, b * P:(b + 1) * P], identity[:])
+            piece, k = divmod(t * P, PIECE)
+            if k == 0:
+                results[piece] = held.tile([P, 4, PIECE], F32, name="result%d" % piece)
+            nc.scalar.copy(results[piece][:, :, k:k + P], back[:])
+
+        windows = [held.tile([P, T], F32, name="window%d" % b) for b in range(4)]
+
+        def scatter(piece, b, values):
+            picked = offsets[:, piece * PIECE // 16:(piece + 1) * PIECE // 16]
+            nc.vector.tensor_copy(windows[b][:].indirect(picked), values)
+
+        def last_expert(piece, b):
+            acc = psum_y.tile([P, 4, P], F32, name="y")
+            y = stage.tile([P, 4, P], F32, name="y_tokens")
+            back = psum_t.tile([P, 4, P], F32, name="yt")
+            for k in range(4):
+                t = piece * 4 + k
+                e = expert_of[t]
+                nc.tensor.matmul_mx(
+                    out=acc[:, k, :],
+                    lhsT=hidden_words[t].bitcast(FP8X4),
+                    lhsT_scale=hidden_scales[t],
+                    rhs=w2[:, e, 2 * b * P:2 * (b + 1) * P].bitcast(FP4X4),
+                    rhs_scale=planes[2][:, e, b * P:(b + 1) * P],
+                    start=True,
+                    stop=True,
+                )
+            for k in range(4):
+                t = piece * 4 + k
+                nc.scalar.activation(y[:, k, :], acc[:, k, :], COPY, scale=gates[:, t:t + 1])
+            for k in range(4):
+                nc.tensor.transpose(back[:, k, :], y[:, k, :], identity[:])
+            values = stage.tile([P, PIECE], F32, name="values")
+            nc.scalar.copy(values[:], back[:].rearrange("p k r -> p (k r)"))
+            scatter(piece, b, values[:])
+
+        for g in range(2):
+            gather(g)
+        for pair in range(8):
+            if pair in (0, 1, 2):
+                gather(pair + 2)
+            first_layer(pair)
+            if 1 <= pair <= 4:
+                second_layer(2 * pair - 2)
+                second_layer(2 * pair - 1)
+            if pair == 5:
+                for b in range(4):
+                    scatter(0, b, results[0][:, b, :])
+        for b in range(4):
+            scatter(1, b, results[1][:, b, :])
+        for b in range(4):
+            last_expert(2, b)
+            last_expert(3, b)
+            nc.sync.dma_start(out[b * P:(b + 1) * P, :], windows[b][:])

@@ -22,10 +22,13 @@ GELU = mybir.ActivationFunctionType.Gelu_apprx_tanh
 MULT = mybir.AluOpType.mult
 
 P = 128
-CHUNK = 512
-VECTOR_COLS = 320
+CHUNKS = (512, 512, 512, 256, 256)
+STARTS = tuple(sum(CHUNKS[:c]) for c in range(len(CHUNKS)))
 GATHERS = (256, 384, 384, 512, 512)
-PIECE = 512
+PIECES = (2, 2, 2, 2)
+VECTOR_TILES = (1, 3, 5, 7)
+ORDER = "G0 G1 F0 G2 F1 G3 F2 S0 C0 G4 F3 S1 C1 F4 S2 C2 F5 S3 C3 F6 F7 L00 L01 L10 L02 L11 L03 L12 L13".split()
+LAST = T - COUNTS[3]
 
 
 def tile_moe_rag_glu_gelu_kernel(
@@ -37,7 +40,7 @@ def tile_moe_rag_glu_gelu_kernel(
 
     with ExitStack() as ctx:
         held = ctx.enter_context(tc.tile_pool(name="held", bufs=1))
-        raws = ctx.enter_context(tc.tile_pool(name="raws", bufs=4))
+        raws = ctx.enter_context(tc.tile_pool(name="raws", bufs=5))
         stage = ctx.enter_context(tc.tile_pool(name="stage", bufs=3))
         psum_ab = ctx.enter_context(tc.psum_pool(name="psum_ab", bufs=2))
         psum_y = ctx.enter_context(tc.psum_pool(name="psum_y", bufs=2))
@@ -46,7 +49,6 @@ def tile_moe_rag_glu_gelu_kernel(
         offsets = held.tile([P, T // 16], U16, name="offsets")
         x_words = held.tile([P, T], U32, name="x_words", align_bytes=64)
         x_scales = held.tile([P, T], U8, name="x_scales", align_bytes=64)
-        nc.gpsimd.memset(x_scales[:], 0)
 
         warm = held.tile([P, 8], F32, name="warm")
         nc.vector.memset(warm[:], 0.0)
@@ -57,14 +59,15 @@ def tile_moe_rag_glu_gelu_kernel(
             plane = held.tile([P, E, H], U8, name="plane_" + name, align_bytes=64)
             nc.vector.memset(plane[:].rearrange("p e n -> p (e n)").bitcast(I32), 0)
             planes.append(plane)
+        nc.vector.memset(x_scales[:].bitcast(I32), 0)
         gate_rows = held.tile([P, P], F32, name="gate_rows")
         nc.vector.memset(gate_rows[:], 0.0)
 
         x_view = xT.rearrange("(p j) w -> p j w", j=4)
         raw_tiles = []
-        for c in range(T // CHUNK):
-            raw = raws.tile([P, 4, CHUNK], F32, name="raw")
-            nc.sync.dma_start(raw[:], x_view[:, :, c * CHUNK:(c + 1) * CHUNK])
+        for c, width in enumerate(CHUNKS):
+            raw = raws.tile([P, 4, width], F32, name="raw")
+            nc.sync.dma_start(raw[:], x_view[:, :, STARTS[c]:STARTS[c] + width])
             raw_tiles.append(raw)
             if c == 1:
                 nc.sync.dma_start(offsets[:], offs)
@@ -72,7 +75,7 @@ def tile_moe_rag_glu_gelu_kernel(
         def load_scales(plane, scales):
             view = scales.rearrange("e s q n -> q (e s) n")
             for quad in range(4):
-                nc.sync.dma_start(
+                nc.gpsimd.dma_start(
                     plane[32 * quad:32 * quad + 4, :, :].bitcast(I32),
                     view[4 * quad:4 * quad + 4, :, :].bitcast(I32),
                 )
@@ -81,31 +84,35 @@ def tile_moe_rag_glu_gelu_kernel(
             view = words.rearrange("e s p n -> p (e s) n")
             nc.sync.dma_start(tile[:, lo:hi, :].bitcast(I32), view[:, lo:hi, :].bitcast(I32))
 
+        gate_wide = held.tile([P, COUNTS[3]], F32, name="gate_wide")
         w1 = held.tile([P, E, 2 * H], U8, name="w1", align_bytes=64)
         w3 = held.tile([P, E, 2 * H], U8, name="w3", align_bytes=64)
         w2 = held.tile([P, E, 2 * N], U8, name="w2", align_bytes=64)
         load_scales(planes[0], w1_scales)
         load_scales(planes[1], w3_scales)
+        load_scales(planes[2], w2_scales)
         load_words(w1, w1_words, 0, 2)
         load_words(w3, w3_words, 0, 2)
+        load_words(w2, w2_words, 0, 2)
         load_words(w1, w1_words, 2, 4)
         load_words(w3, w3_words, 2, 4)
-        load_scales(planes[2], w2_scales)
-        load_words(w2, w2_words, 0, 4)
-        nc.scalar.dma_start(gate_rows[0:tiles, :], gate[0:1, :].rearrange("o (c p) -> (o c) p", p=P))
+        load_words(w2, w2_words, 2, 4)
+        nc.sync.dma_start(gate_wide[:], gate[0:P, LAST:T])
+        nc.gpsimd.dma_start(gate_rows[0:tiles, :], gate[0:1, :].rearrange("o (c p) -> (o c) p", p=P))
 
         identity = held.tile([P, P], F32, name="identity")
         make_identity(nc, identity[:])
 
-        for c in range(T // CHUNK):
+        for c, width in enumerate(CHUNKS):
             raw = raw_tiles[c]
-            grouped = stage.tile([P, CHUNK, 4], BF16, name="grouped", align_bytes=64)
-            for lo, hi, copy in ((0, VECTOR_COLS, nc.vector.tensor_copy), (VECTOR_COLS, CHUNK, nc.scalar.copy)):
+            grouped = stage.tile([P, width, 4], BF16, name="grouped", align_bytes=64)
+            share = width * 5 // 8
+            for lo, hi, copy in ((0, share, nc.vector.tensor_copy), (share, width, nc.scalar.copy)):
                 copy(
                     grouped[:, lo:hi, :].rearrange("p (c i) j -> p c j i", i=4),
                     raw[:, :, lo:hi].rearrange("p j (c i) -> p c j i", i=4),
                 )
-            cols = slice(c * CHUNK, (c + 1) * CHUNK)
+            cols = slice(STARTS[c], STARTS[c] + width)
             nc.vector.quantize_mx(
                 out=x_words[:, cols].bitcast(FP8X4),
                 scales=x_scales[:, cols],
@@ -154,7 +161,12 @@ def tile_moe_rag_glu_gelu_kernel(
                 g = stage.tile([P, H], F32, name="g")
                 nc.scalar.activation(g[:], sums[0][:], GELU)
                 h = stage.tile([P, H], BF16, name="h")
-                nc.vector.tensor_tensor(h[:], g[:], sums[1][:], MULT)
+                if t in VECTOR_TILES:
+                    nc.vector.tensor_tensor(h[:], g[:], sums[1][:], MULT)
+                else:
+                    up = stage.tile([P, H], F32, name="up")
+                    nc.scalar.copy(up[:], sums[1][:])
+                    nc.gpsimd.tensor_tensor(h[:], g[:], up[:], MULT)
                 pairs = h[:].bitcast(F32)
                 for u in range(2):
                     nc.tensor.transpose(turned[:, i, u, :], pairs[:, u::2], identity[:])
@@ -163,12 +175,16 @@ def tile_moe_rag_glu_gelu_kernel(
                 grouped[:].bitcast(F32).rearrange("p (k r u) -> p k r u", k=2, u=2),
                 turned[:].rearrange("p k u r -> p k r u"),
             )
-            words = held.tile([P, 2 * P], U32, name="h_words%d" % pair, align_bytes=64)
-            scales = held.tile([P, 2 * P], U8, name="h_scales%d" % pair, align_bytes=64)
-            nc.vector.quantize_mx(out=words[:].bitcast(FP8X4), scales=scales[:], in_=grouped[:])
-            for i in range(2):
-                hidden_words.append(words[:, i * P:(i + 1) * P])
-                hidden_scales.append(scales[:, i * P:(i + 1) * P])
+            half, at = divmod(2 * pair, 4)
+            if at == 0:
+                hidden_words.append(held.tile([P, 4 * P], U32, name="h_words%d" % half, align_bytes=64))
+                hidden_scales.append(held.tile([P, 4 * P], U8, name="h_scales%d" % half, align_bytes=64))
+            cols = slice(at * P, (at + 2) * P)
+            nc.vector.quantize_mx(
+                out=hidden_words[half][:, cols].bitcast(FP8X4),
+                scales=hidden_scales[half][:, cols],
+                in_=grouped[:],
+            )
 
         results = {}
 
@@ -177,8 +193,8 @@ def tile_moe_rag_glu_gelu_kernel(
             acc = psum_y.tile([P, N], F32, name="y")
             nc.tensor.matmul_mx(
                 out=acc[:],
-                lhsT=hidden_words[t].bitcast(FP8X4),
-                lhsT_scale=hidden_scales[t],
+                lhsT=hidden_words[t // 4][:, t % 4 * P:(t % 4 + 1) * P].bitcast(FP8X4),
+                lhsT_scale=hidden_scales[t // 4][:, t % 4 * P:(t % 4 + 1) * P],
                 rhs=w2[:, e, :].bitcast(FP4X4),
                 rhs_scale=planes[2][:, e, :],
                 start=True,
@@ -189,57 +205,52 @@ def tile_moe_rag_glu_gelu_kernel(
             back = psum_t.tile([P, 4, P], F32, name="yt")
             for b in range(4):
                 nc.tensor.transpose(back[:, b, :], y[:, b * P:(b + 1) * P], identity[:])
-            piece, k = divmod(t * P, PIECE)
+            piece = [i for i in range(len(PIECES)) if sum(PIECES[:i]) <= t][-1]
+            k = (t - sum(PIECES[:piece])) * P
             if k == 0:
-                results[piece] = held.tile([P, 4, PIECE], F32, name="result%d" % piece)
+                results[piece] = held.tile([P, 4, PIECES[piece] * P], F32, name="result%d" % piece)
             nc.scalar.copy(results[piece][:, :, k:k + P], back[:])
 
         windows = [held.tile([P, T], F32, name="window%d" % b) for b in range(4)]
 
-        def scatter(piece, b, values):
-            picked = offsets[:, piece * PIECE // 16:(piece + 1) * PIECE // 16]
-            nc.vector.tensor_copy(windows[b][:].indirect(picked), values)
+        def scatter(piece):
+            lo = sum(PIECES[:piece]) * P // 16
+            picked = offsets[:, lo:lo + PIECES[piece] * P // 16]
+            for b in range(4):
+                nc.vector.tensor_copy(windows[b][:].indirect(picked), results[piece][:, b, :])
 
-        def last_expert(piece, b):
-            acc = psum_y.tile([P, 4, P], F32, name="y")
-            y = stage.tile([P, 4, P], F32, name="y_tokens")
-            back = psum_t.tile([P, 4, P], F32, name="yt")
-            for k in range(4):
-                t = piece * 4 + k
-                e = expert_of[t]
-                nc.tensor.matmul_mx(
-                    out=acc[:, k, :],
-                    lhsT=hidden_words[t].bitcast(FP8X4),
-                    lhsT_scale=hidden_scales[t],
-                    rhs=w2[:, e, 2 * b * P:2 * (b + 1) * P].bitcast(FP4X4),
-                    rhs_scale=planes[2][:, e, b * P:(b + 1) * P],
-                    start=True,
-                    stop=True,
-                )
-            for k in range(4):
-                t = piece * 4 + k
-                nc.scalar.activation(y[:, k, :], acc[:, k, :], COPY, scale=gates[:, t:t + 1])
-            for k in range(4):
-                nc.tensor.transpose(back[:, k, :], y[:, k, :], identity[:])
-            values = stage.tile([P, PIECE], F32, name="values")
-            nc.scalar.copy(values[:], back[:].rearrange("p k r -> p (k r)"))
-            scatter(piece, b, values[:])
+        def last_expert(half, b):
+            acc = psum_y.tile([P, 4 * P], F32, name="y")
+            nc.tensor.matmul_mx(
+                out=acc[:],
+                lhsT=w2[:, 3, 2 * b * P:2 * (b + 1) * P].bitcast(FP4X4),
+                lhsT_scale=planes[2][:, 3, b * P:(b + 1) * P],
+                rhs=hidden_words[2 + half][:].bitcast(FP8X4),
+                rhs_scale=hidden_scales[2 + half][:],
+                start=True,
+                stop=True,
+            )
+            values = stage.tile([P, 4 * P], F32, name="values")
+            nc.scalar.copy(values[:], acc[:])
+            lo = half * 4 * P
+            picked = offsets[:, (LAST + lo) // 16:(LAST + lo + 4 * P) // 16]
+            nc.vector.tensor_tensor(
+                windows[b][:].indirect(picked), values[:], gate_wide[:, lo:lo + 4 * P], MULT
+            )
 
-        for g in range(2):
-            gather(g)
-        for pair in range(8):
-            if pair in (0, 1, 2):
-                gather(pair + 2)
-            first_layer(pair)
-            if 1 <= pair <= 4:
-                second_layer(2 * pair - 2)
-                second_layer(2 * pair - 1)
-            if pair == 5:
-                for b in range(4):
-                    scatter(0, b, results[0][:, b, :])
-        for b in range(4):
-            scatter(1, b, results[1][:, b, :])
-        for b in range(4):
-            last_expert(2, b)
-            last_expert(3, b)
-            nc.sync.dma_start(out[b * P:(b + 1) * P, :], windows[b][:])
+        for item in ORDER:
+            n = int(item[1])
+            if item[0] == "G":
+                gather(n)
+            elif item[0] == "F":
+                first_layer(n)
+            elif item[0] == "S":
+                second_layer(2 * n)
+                second_layer(2 * n + 1)
+            elif item[0] == "C":
+                scatter(n)
+            else:
+                b = int(item[2])
+                last_expert(n, b)
+                if n == 1:
+                    nc.sync.dma_start(out[b * P:(b + 1) * P, :], windows[b][:])

@@ -22,12 +22,14 @@ GELU = mybir.ActivationFunctionType.Gelu_apprx_tanh
 MULT = mybir.AluOpType.mult
 
 P = 128
-CHUNKS = (512, 512, 512, 256, 256)
-STARTS = tuple(sum(CHUNKS[:c]) for c in range(len(CHUNKS)))
+CHUNKS = (1024, 512, 256, 256)
 GATHERS = (256, 384, 384, 512, 512)
 PIECES = (2, 2, 2, 2)
-VECTOR_TILES = (1, 3, 5, 7)
-ORDER = "G0 G1 F0 G2 F1 G3 F2 S0 C0 G4 F3 S1 C1 F4 S2 C2 F5 S3 C3 F6 F7 L00 L01 L10 L02 L11 L03 L12 L13".split()
+TRANSPOSED = ()
+GATED = (0, 1, 2, 3)
+BUFS = 3
+VECTOR_TILES = (3, 4, 5, 6, 7)
+ORDER = "G0 G1 F0 G2 F1 G3 F2 G4 S0 C0 F3 S1 C1 F4 S2 C2 F5 S3 C3 F6 F7 L00 L01 L10 L02 L11 L12 L03 L13".split()
 LAST = T - COUNTS[3]
 
 
@@ -35,13 +37,14 @@ def tile_moe_rag_glu_gelu_kernel(
     tc, xT, w1_words, w1_scales, w3_words, w3_scales, w2_words, w2_scales, gate, offs, out
 ):
     nc = tc.nc
+    STARTS = tuple(sum(CHUNKS[:c]) for c in range(len(CHUNKS)))
     tiles = T // P
     expert_of = [e for e in range(E) for i in range(COUNTS[e] // P)]
 
     with ExitStack() as ctx:
         held = ctx.enter_context(tc.tile_pool(name="held", bufs=1))
         raws = ctx.enter_context(tc.tile_pool(name="raws", bufs=5))
-        stage = ctx.enter_context(tc.tile_pool(name="stage", bufs=3))
+        stage = ctx.enter_context(tc.tile_pool(name="stage", bufs=BUFS))
         psum_ab = ctx.enter_context(tc.psum_pool(name="psum_ab", bufs=2))
         psum_y = ctx.enter_context(tc.psum_pool(name="psum_y", bufs=2))
         psum_t = ctx.enter_context(tc.psum_pool(name="psum_t", bufs=1))
@@ -84,7 +87,7 @@ def tile_moe_rag_glu_gelu_kernel(
             view = words.rearrange("e s p n -> p (e s) n")
             nc.sync.dma_start(tile[:, lo:hi, :].bitcast(I32), view[:, lo:hi, :].bitcast(I32))
 
-        gate_wide = held.tile([P, COUNTS[3]], F32, name="gate_wide")
+        gate_wide = held.tile([P, T], F32, name="gate_wide")
         w1 = held.tile([P, E, 2 * H], U8, name="w1", align_bytes=64)
         w3 = held.tile([P, E, 2 * H], U8, name="w3", align_bytes=64)
         w2 = held.tile([P, E, 2 * N], U8, name="w2", align_bytes=64)
@@ -97,7 +100,7 @@ def tile_moe_rag_glu_gelu_kernel(
         load_words(w1, w1_words, 2, 4)
         load_words(w3, w3_words, 2, 4)
         load_words(w2, w2_words, 2, 4)
-        nc.sync.dma_start(gate_wide[:], gate[0:P, LAST:T])
+        nc.sync.dma_start(gate_wide[:], gate[0:P, :])
         nc.gpsimd.dma_start(gate_rows[0:tiles, :], gate[0:1, :].rearrange("o (c p) -> (o c) p", p=P))
 
         identity = held.tile([P, P], F32, name="identity")
@@ -190,34 +193,51 @@ def tile_moe_rag_glu_gelu_kernel(
 
         def second_layer(t):
             e = expert_of[t]
-            acc = psum_y.tile([P, N], F32, name="y")
-            nc.tensor.matmul_mx(
-                out=acc[:],
-                lhsT=hidden_words[t // 4][:, t % 4 * P:(t % 4 + 1) * P].bitcast(FP8X4),
-                lhsT_scale=hidden_scales[t // 4][:, t % 4 * P:(t % 4 + 1) * P],
-                rhs=w2[:, e, :].bitcast(FP4X4),
-                rhs_scale=planes[2][:, e, :],
-                start=True,
-                stop=True,
-            )
-            y = stage.tile([P, N], F32, name="y_tokens")
-            nc.scalar.activation(y[:], acc[:], COPY, scale=gates[:, t:t + 1])
-            back = psum_t.tile([P, 4, P], F32, name="yt")
-            for b in range(4):
-                nc.tensor.transpose(back[:, b, :], y[:, b * P:(b + 1) * P], identity[:])
-            piece = [i for i in range(len(PIECES)) if sum(PIECES[:i]) <= t][-1]
-            k = (t - sum(PIECES[:piece])) * P
+            words = hidden_words[t // 4][:, t % 4 * P:(t % 4 + 1) * P].bitcast(FP8X4)
+            scales = hidden_scales[t // 4][:, t % 4 * P:(t % 4 + 1) * P]
+            piece, k = divmod(t, 2)
             if k == 0:
-                results[piece] = held.tile([P, 4, PIECES[piece] * P], F32, name="result%d" % piece)
-            nc.scalar.copy(results[piece][:, :, k:k + P], back[:])
+                results[piece] = held.tile([P, 4, 2 * P], F32, name="result%d" % piece)
+            dest = results[piece][:, :, k * P:(k + 1) * P]
+            if piece in TRANSPOSED:
+                acc = psum_y.tile([P, N], F32, name="y")
+                nc.tensor.matmul_mx(
+                    out=acc[:], lhsT=words, lhsT_scale=scales,
+                    rhs=w2[:, e, :].bitcast(FP4X4), rhs_scale=planes[2][:, e, :], start=True, stop=True,
+                )
+                y = stage.tile([P, N], F32, name="y_tokens")
+                nc.scalar.activation(y[:], acc[:], COPY, scale=gates[:, t:t + 1])
+                back = psum_t.tile([P, 4, P], F32, name="yt")
+                for b in range(4):
+                    nc.tensor.transpose(back[:, b, :], y[:, b * P:(b + 1) * P], identity[:])
+                nc.scalar.copy(dest, back[:])
+            else:
+                acc = psum_y.tile([P, 4, P], F32, name="y")
+                for b in range(4):
+                    nc.tensor.matmul_mx(
+                        out=acc[:, b, :],
+                        lhsT=w2[:, e, 2 * b * P:2 * (b + 1) * P].bitcast(FP4X4),
+                        lhsT_scale=planes[2][:, e, b * P:(b + 1) * P],
+                        rhs=words, rhs_scale=scales, start=True, stop=True,
+                    )
+                nc.scalar.copy(dest, acc[:])
+                if piece in GATED:
+                    nc.gpsimd.tensor_tensor(
+                        dest, dest, gate_wide[:, t * P:(t + 1) * P].unsqueeze(1).to_broadcast([P, 4, P]), MULT
+                    )
 
         windows = [held.tile([P, T], F32, name="window%d" % b) for b in range(4)]
 
         def scatter(piece):
-            lo = sum(PIECES[:piece]) * P // 16
-            picked = offsets[:, lo:lo + PIECES[piece] * P // 16]
+            lo = piece * 2 * P
+            picked = offsets[:, lo // 16:(lo + 2 * P) // 16]
             for b in range(4):
-                nc.vector.tensor_copy(windows[b][:].indirect(picked), results[piece][:, b, :])
+                if piece in TRANSPOSED or piece in GATED:
+                    nc.vector.tensor_copy(windows[b][:].indirect(picked), results[piece][:, b, :])
+                else:
+                    nc.vector.tensor_tensor(
+                        windows[b][:].indirect(picked), results[piece][:, b, :], gate_wide[:, lo:lo + 2 * P], MULT
+                    )
 
         def last_expert(half, b):
             acc = psum_y.tile([P, 4 * P], F32, name="y")
@@ -234,9 +254,12 @@ def tile_moe_rag_glu_gelu_kernel(
             nc.scalar.copy(values[:], acc[:])
             lo = half * 4 * P
             picked = offsets[:, (LAST + lo) // 16:(LAST + lo + 4 * P) // 16]
-            nc.vector.tensor_tensor(
-                windows[b][:].indirect(picked), values[:], gate_wide[:, lo:lo + 4 * P], MULT
-            )
+            gates_here = gate_wide[:, LAST + lo:LAST + lo + 4 * P]
+            if 4 + half in GATED:
+                nc.gpsimd.tensor_tensor(values[:], values[:], gates_here, MULT)
+                nc.vector.tensor_copy(windows[b][:].indirect(picked), values[:])
+            else:
+                nc.vector.tensor_tensor(windows[b][:].indirect(picked), values[:], gates_here, MULT)
 
         for item in ORDER:
             n = int(item[1])

@@ -22,14 +22,15 @@ GELU = mybir.ActivationFunctionType.Gelu_apprx_tanh
 MULT = mybir.AluOpType.mult
 
 P = 128
-CHUNKS = (1024, 512, 256, 256)
+CHUNKS = (512, 512, 512, 256, 256)
 GATHERS = (256, 384, 384, 512, 512)
 PIECES = (2, 2, 2, 2)
-TRANSPOSED = ()
-GATED = (0, 1, 2, 3)
+TRANSPOSED = (0, 1, 2, 3)
 BUFS = 3
-VECTOR_TILES = (3, 4, 5, 6, 7)
-ORDER = "G0 G1 F0 G2 F1 G3 F2 G4 S0 C0 F3 S1 C1 F4 S2 C2 F5 S3 C3 F6 F7 L00 L01 L10 L02 L11 L12 L03 L13".split()
+SLOTBUFS = 2
+GATED = ()
+VECTOR_TILES = (0, 1, 2, 3, 4, 5, 6, 7)
+ORDER = "G0 G1 F0 G2 F1 F2 G3 S0 C0 F3 G4 S1 C1 F4 S2 C2 F5 S3 C3 F6 F7 L00 L01 L10 L02 L11 L03 L12 L13".split()
 LAST = T - COUNTS[3]
 
 
@@ -44,6 +45,7 @@ def tile_moe_rag_glu_gelu_kernel(
     with ExitStack() as ctx:
         held = ctx.enter_context(tc.tile_pool(name="held", bufs=1))
         raws = ctx.enter_context(tc.tile_pool(name="raws", bufs=5))
+        slots = ctx.enter_context(tc.tile_pool(name="slots", bufs=SLOTBUFS))
         stage = ctx.enter_context(tc.tile_pool(name="stage", bufs=BUFS))
         psum_ab = ctx.enter_context(tc.psum_pool(name="psum_ab", bufs=2))
         psum_y = ctx.enter_context(tc.psum_pool(name="psum_y", bufs=2))
@@ -75,10 +77,10 @@ def tile_moe_rag_glu_gelu_kernel(
             if c == 1:
                 nc.sync.dma_start(offsets[:], offs)
 
-        def load_scales(plane, scales):
+        def load_scales(queue, plane, scales):
             view = scales.rearrange("e s q n -> q (e s) n")
             for quad in range(4):
-                nc.gpsimd.dma_start(
+                queue.dma_start(
                     plane[32 * quad:32 * quad + 4, :, :].bitcast(I32),
                     view[4 * quad:4 * quad + 4, :, :].bitcast(I32),
                 )
@@ -91,17 +93,17 @@ def tile_moe_rag_glu_gelu_kernel(
         w1 = held.tile([P, E, 2 * H], U8, name="w1", align_bytes=64)
         w3 = held.tile([P, E, 2 * H], U8, name="w3", align_bytes=64)
         w2 = held.tile([P, E, 2 * N], U8, name="w2", align_bytes=64)
-        load_scales(planes[0], w1_scales)
-        load_scales(planes[1], w3_scales)
-        load_scales(planes[2], w2_scales)
+        load_scales(nc.gpsimd, planes[0], w1_scales)
+        load_scales(nc.gpsimd, planes[1], w3_scales)
         load_words(w1, w1_words, 0, 2)
         load_words(w3, w3_words, 0, 2)
         load_words(w2, w2_words, 0, 2)
+        load_scales(nc.sync, planes[2], w2_scales)
+        nc.sync.dma_start(gate_rows[0:tiles, :], gate[0:1, :].rearrange("o (c p) -> (o c) p", p=P))
         load_words(w1, w1_words, 2, 4)
         load_words(w3, w3_words, 2, 4)
         load_words(w2, w2_words, 2, 4)
         nc.sync.dma_start(gate_wide[:], gate[0:P, :])
-        nc.gpsimd.dma_start(gate_rows[0:tiles, :], gate[0:1, :].rearrange("o (c p) -> (o c) p", p=P))
 
         identity = held.tile([P, P], F32, name="identity")
         make_identity(nc, identity[:])
@@ -132,8 +134,8 @@ def tile_moe_rag_glu_gelu_kernel(
         def gather(g):
             lo = sum(GATHERS[:g])
             n = GATHERS[g]
-            words = held.tile([P, n], U32, name="slot_words%d" % g, align_bytes=64)
-            scales = held.tile([P, n], U8, name="slot_scales%d" % g, align_bytes=64)
+            words = slots.tile([P, n], U32, name="slot_words", align_bytes=64)
+            scales = slots.tile([P, n], U8, name="slot_scales", align_bytes=64)
             picked = offsets[:, lo // 16:(lo + n) // 16]
             nc.vector.tensor_copy(words[:], x_words[:].indirect(picked))
             nc.vector.tensor_copy(scales[:], x_scales[:].indirect(picked))
@@ -254,12 +256,9 @@ def tile_moe_rag_glu_gelu_kernel(
             nc.scalar.copy(values[:], acc[:])
             lo = half * 4 * P
             picked = offsets[:, (LAST + lo) // 16:(LAST + lo + 4 * P) // 16]
-            gates_here = gate_wide[:, LAST + lo:LAST + lo + 4 * P]
-            if 4 + half in GATED:
-                nc.gpsimd.tensor_tensor(values[:], values[:], gates_here, MULT)
-                nc.vector.tensor_copy(windows[b][:].indirect(picked), values[:])
-            else:
-                nc.vector.tensor_tensor(windows[b][:].indirect(picked), values[:], gates_here, MULT)
+            nc.vector.tensor_tensor(
+                windows[b][:].indirect(picked), values[:], gate_wide[:, LAST + lo:LAST + lo + 4 * P], MULT
+            )
 
         for item in ORDER:
             n = int(item[1])

from contextlib import ExitStack

import concourse.mybir as mybir
from concourse.masks import make_identity

K, T, E, H, N = 512, 2048, 4, 512, 512
COUNTS = (128, 256, 640, 1024)

FLOPS = 3 * 2 * K * H * T
BYTES = 4 * K * T + 3 * E * (K * H // 2 + K * H // 32) + 4 * T + 2 * T * 8 + 4 * N * T

F32 = mybir.dt.float32
BF16 = mybir.dt.bfloat16
I32 = mybir.dt.int32
U32 = mybir.dt.uint32
U16 = mybir.dt.uint16
U8 = mybir.dt.uint8
FP8X4 = mybir.dt.float8_e4m3fn_x4
FP4X4 = mybir.dt.float4_e2m1fn_x4
COPY = mybir.ActivationFunctionType.Copy
GELU = mybir.ActivationFunctionType.Gelu_apprx_tanh
MULT = mybir.AluOpType.mult

P = 128
CHUNKS = (512, 512, 512, 256, 256)
GATHERS = (256, 384, 384, 512, 512)
PIECES = (2, 2, 2, 2)
TRANSPOSED = (0, 1, 2, 3)
BUFS = 3
SLOTBUFS = 2
GATED = ()
VECTOR_TILES = (0, 1, 2, 3, 4, 5, 6, 7)
ORDER = "G0 G1 F0 G2 F1 F2 G3 S0 C0 F3 G4 S1 C1 F4 S2 C2 F5 S3 C3 F6 F7 L00 L01 L10 L02 L11 L03 L12 L13".split()
LAST = T - COUNTS[3]


def tile_moe_rag_glu_gelu_kernel(
    tc, xT, w1_words, w1_scales, w3_words, w3_scales, w2_words, w2_scales, gate, offs, out
):
    nc = tc.nc
    STARTS = tuple(sum(CHUNKS[:c]) for c in range(len(CHUNKS)))
    tiles = T // P
    expert_of = [e for e in range(E) for i in range(COUNTS[e] // P)]

    with ExitStack() as ctx:
        held = ctx.enter_context(tc.tile_pool(name="held", bufs=1))
        raws = ctx.enter_context(tc.tile_pool(name="raws", bufs=5))
        slots = ctx.enter_context(tc.tile_pool(name="slots", bufs=SLOTBUFS))
        stage = ctx.enter_context(tc.tile_pool(name="stage", bufs=BUFS))
        psum_ab = ctx.enter_context(tc.psum_pool(name="psum_ab", bufs=2))
        psum_y = ctx.enter_context(tc.psum_pool(name="psum_y", bufs=2))
        psum_t = ctx.enter_context(tc.psum_pool(name="psum_t", bufs=1))

        offsets = held.tile([P, T // 16], U16, name="offsets")
        x_words = held.tile([P, T], U32, name="x_words", align_bytes=64)
        x_scales = held.tile([P, T], U8, name="x_scales", align_bytes=64)

        warm = held.tile([P, 8], F32, name="warm")
        nc.vector.memset(warm[:], 0.0)
        nc.scalar.activation(warm[:, 0:1], warm[:, 1:2], GELU)

        planes = []
        for name in ("w1", "w3", "w2"):
            plane = held.tile([P, E, H], U8, name="plane_" + name, align_bytes=64)
            nc.vector.memset(plane[:].rearrange("p e n -> p (e n)").bitcast(I32), 0)
            planes.append(plane)
        nc.vector.memset(x_scales[:].bitcast(I32), 0)
        gate_rows = held.tile([P, P], F32, name="gate_rows")
        nc.vector.memset(gate_rows[:], 0.0)

        x_view = xT.rearrange("(p j) w -> p j w", j=4)
        raw_tiles = []
        for c, width in enumerate(CHUNKS):
            raw = raws.tile([P, 4, width], F32, name="raw")
            nc.sync.dma_start(raw[:], x_view[:, :, STARTS[c]:STARTS[c] + width])
            raw_tiles.append(raw)
            if c == 1:
                nc.sync.dma_start(offsets[:], offs)

        def load_scales(queue, plane, scales):
            view = scales.rearrange("e s q n -> q (e s) n")
            for quad in range(4):
                queue.dma_start(
                    plane[32 * quad:32 * quad + 4, :, :].bitcast(I32),
                    view[4 * quad:4 * quad + 4, :, :].bitcast(I32),
                )

        def load_words(tile, words, lo, hi):
            view = words.rearrange("e s p n -> p (e s) n")
            nc.sync.dma_start(tile[:, lo:hi, :].bitcast(I32), view[:, lo:hi, :].bitcast(I32))

        gate_wide = held.tile([P, T], F32, name="gate_wide")
        w1 = held.tile([P, E, 2 * H], U8, name="w1", align_bytes=64)
        w3 = held.tile([P, E, 2 * H], U8, name="w3", align_bytes=64)
        w2 = held.tile([P, E, 2 * N], U8, name="w2", align_bytes=64)
        load_scales(nc.gpsimd, planes[0], w1_scales)
        load_scales(nc.gpsimd, planes[1], w3_scales)
        load_words(w1, w1_words, 0, 2)
        load_words(w3, w3_words, 0, 2)
        load_words(w2, w2_words, 0, 2)
        load_scales(nc.sync, planes[2], w2_scales)
        nc.sync.dma_start(gate_rows[0:tiles, :], gate[0:1, :].rearrange("o (c p) -> (o c) p", p=P))
        load_words(w1, w1_words, 2, 4)
        load_words(w3, w3_words, 2, 4)
        load_words(w2, w2_words, 2, 4)
        nc.sync.dma_start(gate_wide[:], gate[0:P, :])

        identity = held.tile([P, P], F32, name="identity")
        make_identity(nc, identity[:])

        for c, width in enumerate(CHUNKS):
            raw = raw_tiles[c]
            grouped = stage.tile([P, width, 4], BF16, name="grouped", align_bytes=64)
            share = width * 5 // 8
            for lo, hi, copy in ((0, share, nc.vector.tensor_copy), (share, width, nc.scalar.copy)):
                copy(
                    grouped[:, lo:hi, :].rearrange("p (c i) j -> p c j i", i=4),
                    raw[:, :, lo:hi].rearrange("p j (c i) -> p c j i", i=4),
                )
            cols = slice(STARTS[c], STARTS[c] + width)
            nc.vector.quantize_mx(
                out=x_words[:, cols].bitcast(FP8X4),
                scales=x_scales[:, cols],
                in_=grouped[:].rearrange("p w j -> p (w j)"),
            )

        gate_psum = psum_t.tile([P, P], F32, name="yt")
        nc.tensor.transpose(gate_psum[:], gate_rows[:], identity[:])
        gates = held.tile([P, tiles], F32, name="gates")
        nc.vector.tensor_copy(gates[:], gate_psum[:, 0:tiles])

        slot_words, slot_scales = [], []

        def gather(g):
            lo = sum(GATHERS[:g])
            n = GATHERS[g]
            words = slots.tile([P, n], U32, name="slot_words", align_bytes=64)
            scales = slots.tile([P, n], U8, name="slot_scales", align_bytes=64)
            picked = offsets[:, lo // 16:(lo + n) // 16]
            nc.vector.tensor_copy(words[:], x_words[:].indirect(picked))
            nc.vector.tensor_copy(scales[:], x_scales[:].indirect(picked))
            for k in range(n // P):
                slot_words.append(words[:, k * P:(k + 1) * P])
                slot_scales.append(scales[:, k * P:(k + 1) * P])

        hidden_words, hidden_scales = [], []

        def first_layer(pair):
            turned = psum_t.tile([P, 2, 2, P], F32, name="ht")
            for i in range(2):
                t = 2 * pair + i
                e = expert_of[t]
                sums = []
                for w, plane, name in ((w1, planes[0], "a"), (w3, planes[1], "b")):
                    acc = psum_ab.tile([P, H], F32, name=name)
                    nc.tensor.matmul_mx(
                        out=acc[:],
                        lhsT=slot_words[t].bitcast(FP8X4),
                        lhsT_scale=slot_scales[t],
                        rhs=w[:, e, :].bitcast(FP4X4),
                        rhs_scale=plane[:, e, :],
                        start=True,
                        stop=True,
                    )
                    sums.append(acc)
                g = stage.tile([P, H], F32, name="g")
                nc.scalar.activation(g[:], sums[0][:], GELU)
                h = stage.tile([P, H], BF16, name="h")
                if t in VECTOR_TILES:
                    nc.vector.tensor_tensor(h[:], g[:], sums[1][:], MULT)
                else:
                    up = stage.tile([P, H], F32, name="up")
                    nc.scalar.copy(up[:], sums[1][:])
                    nc.gpsimd.tensor_tensor(h[:], g[:], up[:], MULT)
                pairs = h[:].bitcast(F32)
                for u in range(2):
                    nc.tensor.transpose(turned[:, i, u, :], pairs[:, u::2], identity[:])
            grouped = stage.tile([P, 2 * P * 4], BF16, name="hg", align_bytes=64)
            nc.scalar.copy(
                grouped[:].bitcast(F32).rearrange("p (k r u) -> p k r u", k=2, u=2),
                turned[:].rearrange("p k u r -> p k r u"),
            )
            half, at = divmod(2 * pair, 4)
            if at == 0:
                hidden_words.append(held.tile([P, 4 * P], U32, name="h_words%d" % half, align_bytes=64))
                hidden_scales.append(held.tile([P, 4 * P], U8, name="h_scales%d" % half, align_bytes=64))
            cols = slice(at * P, (at + 2) * P)
            nc.vector.quantize_mx(
                out=hidden_words[half][:, cols].bitcast(FP8X4),
                scales=hidden_scales[half][:, cols],
                in_=grouped[:],
            )

        results = {}

        def second_layer(t):
            e = expert_of[t]
            words = hidden_words[t // 4][:, t % 4 * P:(t % 4 + 1) * P].bitcast(FP8X4)
            scales = hidden_scales[t // 4][:, t % 4 * P:(t % 4 + 1) * P]
            piece, k = divmod(t, 2)
            if k == 0:
                results[piece] = held.tile([P, 4, 2 * P], F32, name="result%d" % piece)
            dest = results[piece][:, :, k * P:(k + 1) * P]
            if piece in TRANSPOSED:
                acc = psum_y.tile([P, N], F32, name="y")
                nc.tensor.matmul_mx(
                    out=acc[:], lhsT=words, lhsT_scale=scales,
                    rhs=w2[:, e, :].bitcast(FP4X4), rhs_scale=planes[2][:, e, :], start=True, stop=True,
                )
                y = stage.tile([P, N], F32, name="y_tokens")
                nc.scalar.activation(y[:], acc[:], COPY, scale=gates[:, t:t + 1])
                back = psum_t.tile([P, 4, P], F32, name="yt")
                for b in range(4):
                    nc.tensor.transpose(back[:, b, :], y[:, b * P:(b + 1) * P], identity[:])
                nc.scalar.copy(dest, back[:])
            else:
                acc = psum_y.tile([P, 4, P], F32, name="y")
                for b in range(4):
                    nc.tensor.matmul_mx(
                        out=acc[:, b, :],
                        lhsT=w2[:, e, 2 * b * P:2 * (b + 1) * P].bitcast(FP4X4),
                        lhsT_scale=planes[2][:, e, b * P:(b + 1) * P],
                        rhs=words, rhs_scale=scales, start=True, stop=True,
                    )
                nc.scalar.copy(dest, acc[:])
                if piece in GATED:
                    nc.gpsimd.tensor_tensor(
                        dest, dest, gate_wide[:, t * P:(t + 1) * P].unsqueeze(1).to_broadcast([P, 4, P]), MULT
                    )

        windows = [held.tile([P, T], F32, name="window%d" % b) for b in range(4)]

        def scatter(piece):
            lo = piece * 2 * P
            picked = offsets[:, lo // 16:(lo + 2 * P) // 16]
            for b in range(4):
                if piece in TRANSPOSED or piece in GATED:
                    nc.vector.tensor_copy(windows[b][:].indirect(picked), results[piece][:, b, :])
                else:
                    nc.vector.tensor_tensor(
                        windows[b][:].indirect(picked), results[piece][:, b, :], gate_wide[:, lo:lo + 2 * P], MULT
                    )

        def last_expert(half, b):
            acc = psum_y.tile([P, 4 * P], F32, name="y")
            nc.tensor.matmul_mx(
                out=acc[:],
                lhsT=w2[:, 3, 2 * b * P:2 * (b + 1) * P].bitcast(FP4X4),
                lhsT_scale=planes[2][:, 3, b * P:(b + 1) * P],
                rhs=hidden_words[2 + half][:].bitcast(FP8X4),
                rhs_scale=hidden_scales[2 + half][:],
                start=True,
                stop=True,
            )
            values = stage.tile([P, 4 * P], F32, name="values")
            nc.scalar.copy(values[:], acc[:])
            lo = half * 4 * P
            picked = offsets[:, (LAST + lo) // 16:(LAST + lo + 4 * P) // 16]
            nc.vector.tensor_tensor(
                windows[b][:].indirect(picked), values[:], gate_wide[:, LAST + lo:LAST + lo + 4 * P], MULT
            )

        for item in ORDER:
            n = int(item[1])
            if item[0] == "G":
                gather(n)
            elif item[0] == "F":
                first_layer(n)
            elif item[0] == "S":
                second_layer(2 * n)
                second_layer(2 * n + 1)
            elif item[0] == "C":
                scatter(n)
            else:
                b = int(item[2])
                last_expert(n, b)
                if n == 1:
                    nc.sync.dma_start(out[b * P:(b + 1) * P, :], windows[b][:])
